import numpy as np
import ml_dtypes


def mxq(x, axis, fmt="e4m3"):
    dtype, down = {"e4m3": (ml_dtypes.float8_e4m3fn, 7), "e5m2": (ml_dtypes.float8_e5m2, 14)}[fmt]
    v = np.moveaxis(np.asarray(x, np.float32).astype(ml_dtypes.bfloat16).astype(np.float64), axis, -1)
    blocks = v.reshape(v.shape[:-1] + (-1, 32))
    amax = np.abs(blocks).max(-1, keepdims=True)
    byte = np.maximum(np.where(amax > 0, np.frexp(amax)[1] - 1 + 127, 0) - down, 1)
    scale = np.exp2(byte - 127.0)
    codes = (blocks / scale).astype(np.float32).astype(dtype).astype(np.float64)
    return np.moveaxis((codes * scale).reshape(v.shape), -1, axis)


WIDE = False


def mx_kscale(k):
    if not WIDE:
        return np.ones(k)
    levels = np.array([10, -10, 5, -5, 0])
    if k % 512:
        return np.exp2(np.random.permutation(np.resize(levels, k // 32))).repeat(32)
    a = np.empty((k // 512, 16))
    for p in range(k // 512):
        a[p, :8] = np.random.permutation(np.resize(levels, 8))
        for g in range(8):
            far = levels[np.abs(levels - a[p, g]) >= 10]
            a[p, g + 8] = far[np.random.randint(len(far))]
    return np.exp2(a.ravel()).repeat(32)


def f64(x):
    return np.asarray(x).astype(np.float64)


def striped(idx):
    return np.tile(idx.reshape(-1, 16).T, (8, 1)).astype(np.uint16)


def unstriped(offs):
    return offs[:16].T.reshape(-1).astype(np.int64)


def striped8(idx):
    return np.concatenate([x.reshape(-1, 16).T for x in idx]).astype(np.uint16)


def runs(offs, k):
    lists = np.stack([offs[16 * r : 16 * r + 16].T.reshape(-1) for r in range(8)]).astype(np.int64)
    return lists[np.arange(k) % 512 // 64]


def pack_weight(w):
    k, n = w.shape
    w = f64(np.asarray(w, np.float32).astype(ml_dtypes.bfloat16)).reshape(k // 32, 32, n)
    amax = np.abs(w).max(1)
    byte = np.clip(np.where(amax > 0, np.frexp(amax)[1] - 1 + 127 - 7, 1), 1, 254)
    scaled = (w * np.exp2(127.0 - byte)[:, None, :]).reshape(k, n).astype(np.float32)
    words = np.ascontiguousarray(scaled.reshape(k // 512, 128, 4, n).transpose(0, 1, 3, 2)).astype(ml_dtypes.float8_e4m3fn).view(np.uint8)
    return words, np.ascontiguousarray(byte.astype(np.uint8).reshape(k // 512, 16, n))


def unpack_weight(words, scales):
    g, p, n, _ = words.shape
    vals = np.ascontiguousarray(words).view(ml_dtypes.float8_e4m3fn).astype(np.float64) * np.repeat(np.exp2(scales.astype(np.float64) - 127.0), 8, axis=1)[..., None]
    return vals.transpose(0, 1, 3, 2).reshape(g * 512, n)


def relu(v):
    return np.maximum(v, 0.0)

def planes(y):
    n, m = y.shape
    v = y.astype(np.float32).astype(ml_dtypes.bfloat16).astype(np.float64).reshape(n // 32, 32, m)
    top = np.abs(v).max(1)
    byte = np.clip(np.where(top > 0, np.frexp(top)[1] - 1 + 127 - 7, 1), 1, 254)
    codes = (v * np.exp2(127.0 - byte)[:, None, :]).reshape(n, m).astype(np.float32).astype(ml_dtypes.float8_e4m3fn).view(np.uint8)
    words = codes.reshape(n // 512, 128, 4, m).transpose(0, 1, 3, 2)
    return np.ascontiguousarray(words), np.ascontiguousarray(byte.astype(np.uint8).reshape(n // 512, 16, m))


K, T, S, N, H = 512, 2048, 512, 512, 512
P = 2 ** 7


def setup_inputs():
    n = np.random.standard_normal
    s = mx_kscale(K)[:, None]
    u = mx_kscale(S)
    packed_xT = pack_weight(n((K, T)) * s)
    packed_w1 = pack_weight(n((S, N)) / np.sqrt(S) / u[:, None])
    return {
        "x_words": packed_xT[0],
        "x_scales": packed_xT[1],
        "wa": (n((K, H)) / np.sqrt(K) / s).astype(np.float32),
        "c1": np.tile(np.random.uniform(0.3, 0.9, H), (P, 1)).astype(np.float32),
        "c2": np.tile(np.random.uniform(0.3, 0.9, H), (P, 1)).astype(np.float32),
        "c3": np.tile(np.random.uniform(0.3, 0.9, H), (P, 1)).astype(np.float32),
        "gt": (np.random.uniform(0.5, 1.5, (S, 1)) * u[:, None]).astype(np.float32),
        "w1_words": packed_w1[0],
        "w1_scales": packed_w1[1],
        "offs": striped(np.random.permutation(T)[:S]),
        "f1": striped8(np.stack([np.random.permutation(H) for _ in range(8)])),
        "f2": striped8(np.stack([np.random.permutation(H) for _ in range(8)])),
        "f3": striped8(np.stack([np.random.permutation(H) for _ in range(8)])),
    }


def reference(x_words, x_scales, wa, c1, c2, c3, gt, w1_words, w1_scales, offs, f1, f2, f3):
    xq = unpack_weight(x_words, x_scales)[:, unstriped(offs)]
    y = xq.T @ mxq(f64(wa), 0, "e4m3")
    z = f64(gt) * (relu(f64(c1)[:1] * (y[np.arange(S)[:, None], runs(f1, S)]) + f64(c2)[:1] * (y[np.arange(S)[:, None], runs(f2, S)]) + f64(c3)[:1] * (y[np.arange(S)[:, None], runs(f3, S)])))
    out_0 = unpack_weight(w1_words, w1_scales).T @ mxq(z, 0, "e4m3")
    return (out_0,) + planes(out_0)

@@ -1,0 +1,220 @@
+from contextlib import ExitStack
+
+import concourse.mybir as mybir
+from concourse.masks import make_identity
+
+F32 = mybir.dt.float32
+BF16 = mybir.dt.bfloat16
+I32 = mybir.dt.int32
+U32 = mybir.dt.uint32
+U16 = mybir.dt.uint16
+U8 = mybir.dt.uint8
+FP8X4 = mybir.dt.float8_e4m3fn_x4
+MULT = mybir.AluOpType.mult
+RELU = mybir.ActivationFunctionType.Relu
+COPY = mybir.ActivationFunctionType.Copy
+
+P = 128
+PACK = 4
+T = 2048
+S = 512
+H = 512
+FLOPS = 2 * 2 * 512 * 512 * 512
+
+WA_PIECES = ((0, 256), (256, 128), (384, 128))
+STAGES = ((0, 256), (256, 128), (384, 128))
+
+
+def tile_picked_feattap_relu_po_kernel(
+    tc, x_words, x_scales, wa, c1, c2, c3, gt, w1_words, w1_scales, offs, f1, f2, f3, out_0, out_1, out_2
+):
+    nc = tc.nc
+    with ExitStack() as ctx:
+        keep = ctx.enter_context(tc.tile_pool(name="keep", bufs=1))
+        ring = ctx.enter_context(tc.tile_pool(name="ring", bufs=2))
+        psum = ctx.enter_context(tc.psum_pool(name="psum", bufs=2))
+
+        picks = keep.tile([P, S // 16], U16, name="picks")
+        taps = [keep.tile([P, H // 16], U16, name=f"taps{k}") for k in range(3)]
+        x_w = keep.tile([P, T], U32, name="x_w", align_bytes=64)
+        x_s = keep.tile([P, T], U8, name="x_s", align_bytes=64)
+        w1_w = keep.tile([P, S], I32, name="w1_w", align_bytes=64)
+        w1_s = keep.tile([P, S], U8, name="w1_s", align_bytes=64)
+        coef = [keep.tile([P, H], F32, name=f"coef{k}") for k in range(3)]
+        gate = keep.tile([P, PACK], F32, name="gate")
+        ident = keep.tile([P, P], F32, name="ident")
+        wa_raw = [keep.tile([P, PACK, w], F32, name=f"wa_raw{i}") for i, (j0, w) in enumerate(WA_PIECES)]
+
+        nc.gpsimd.memset(x_s[:].bitcast(I32), 0)
+        nc.vector.memset(w1_s[:].bitcast(I32), 0)
+        make_identity(nc, ident[:])
+
+        nc.sync.dma_start(picks[:], offs)
+        for q in range(4):
+            nc.sync.dma_start(x_s[32 * q : 32 * q + 4, :].bitcast(I32), x_scales[0][4 * q : 4 * q + 4, :].bitcast(I32))
+        nc.sync.dma_start(x_w[:].bitcast(I32), x_words[0].rearrange("p n t -> p (n t)").bitcast(I32))
+        wa_rows = wa.rearrange("(p j) n -> p j n", j=PACK)
+        for i, (j0, w) in enumerate(WA_PIECES):
+            nc.sync.dma_start(wa_raw[i][:], wa_rows[:, :, j0 : j0 + w])
+        nc.sync.dma_start(w1_w[:], w1_words[0].rearrange("p n t -> p (n t)").bitcast(I32))
+        for q in range(4):
+            nc.gpsimd.dma_start(w1_s[32 * q : 32 * q + 4, :].bitcast(I32), w1_scales[0][4 * q : 4 * q + 4, :].bitcast(I32))
+        for k, (f, c) in enumerate(((f1, c1), (f2, c2), (f3, c3))):
+            nc.sync.dma_start(taps[k][:], f)
+            nc.sync.dma_start(coef[k][:], c)
+        nc.gpsimd.dma_start(gate[:], gt.rearrange("(p t) o -> p (t o)", t=PACK))
+
+        xs_picked = keep.tile([P, S], U8, name="xs_picked", align_bytes=64)
+        xs_dealt = keep.tile([P, S], U8, name="xs_dealt", align_bytes=64)
+        xw_dealt = keep.tile([P, S], U32, name="xw_dealt", align_bytes=64)
+        nc.vector.tensor_copy(xs_picked[:], x_s[:].indirect(picks[:]))
+        nc.vector.tensor_copy(
+            xs_dealt[:].rearrange("p (t m) -> p t m", t=PACK), xs_picked[:].rearrange("p (m t) -> p t m", t=PACK)
+        )
+        nc.vector.tensor_copy(xw_dealt[:].rearrange("p (t m) -> p m t", t=PACK), x_w[:].indirect(picks[:]))
+
+        wa_codes = keep.tile([P, H], U32, name="wa_codes", align_bytes=64)
+        wa_s = keep.tile([P, H], U8, name="wa_s", align_bytes=64)
+        wa_b = [keep.tile([P, w, PACK], BF16, name=f"wa_b{i}", align_bytes=64) for i, (j0, w) in enumerate(WA_PIECES)]
+        nc.scalar.copy(wa_b[0][:], wa_raw[0][:].rearrange("p j w -> p w j"))
+        for i in (1, 2):
+            nc.vector.tensor_copy(wa_b[i][:], wa_raw[i][:].rearrange("p j w -> p w j"))
+        for i, (j0, w) in enumerate(WA_PIECES):
+            nc.vector.quantize_mx(
+                out=wa_codes[:, j0 : j0 + w].bitcast(FP8X4),
+                scales=wa_s[:, j0 : j0 + w],
+                in_=wa_b[i][:].rearrange("p w j -> p (w j)"),
+            )
+
+        y = [keep.tile([P, H], F32, name=f"y{t}") for t in range(PACK)]
+        for t in range(PACK):
+            y_bank = psum.tile([P, H], F32, name="y_bank")
+            rows = slice(P * t, P * (t + 1))
+            for j0, w in WA_PIECES if t == 0 else ((0, H),):
+                nc.tensor.matmul_mx(
+                    out=y_bank[:, j0 : j0 + w],
+                    lhsT=xw_dealt[:, rows].bitcast(FP8X4),
+                    lhsT_scale=xs_dealt[:, rows],
+                    rhs=wa_codes[:, j0 : j0 + w].bitcast(FP8X4),
+                    rhs_scale=wa_s[:, j0 : j0 + w],
+                    start=True,
+                    stop=True,
+                )
+            nc.scalar.copy(y[t][:], y_bank[:])
+
+        w1w_dealt = keep.tile([P, S], I32, name="w1w_dealt", align_bytes=64)
+        w1s_dealt = keep.tile([P, S], U8, name="w1s_dealt", align_bytes=64)
+        nc.vector.tensor_copy(
+            w1w_dealt[:].rearrange("p (t m) -> p t m", t=PACK), w1_w[:].rearrange("p (m t) -> p t m", t=PACK)
+        )
+        nc.vector.tensor_copy(
+            w1s_dealt[:].rearrange("p (t m) -> p t m", t=PACK), w1_s[:].rearrange("p (m t) -> p t m", t=PACK)
+        )
+
+        z_codes = keep.tile([P, H], U32, name="z_codes", align_bytes=64)
+        z_s = keep.tile([P, H], U8, name="z_s", align_bytes=64)
+        o_codes = keep.tile([P, H], U32, name="o_codes", align_bytes=64)
+        o_s = keep.tile([P, H], U8, name="o_s", align_bytes=64)
+        out_rows = out_0.rearrange("(p t) n -> p t n", t=PACK)
+        out_words = out_1[0].rearrange("p n t -> p (n t)").bitcast(I32)
+
+        def sum_taps(j0, w, t):
+            terms = []
+            for k in range(3):
+                term = ring.tile([P, w], F32, name="term", bufs=6)
+                nc.vector.tensor_tensor(
+                    term[:], y[t][:].indirect(taps[k][:, j0 // 16 : (j0 + w) // 16]), coef[k][:, j0 : j0 + w], MULT
+                )
+                terms.append(term)
+            turned = psum.tile([P, w], F32, name="turned")
+            for b in range(0, w, P):
+                for k in range(3):
+                    nc.tensor.matmul(
+                        turned[:, b : b + P],
+                        terms[k][:, b : b + P],
+                        ident[:],
+                        start=(k == 0),
+                        stop=(k == 2),
+                        is_transpose=True,
+                    )
+            rectified = ring.tile([P, w], F32, name="rectified")
+            nc.scalar.activation(rectified[:], turned[:], RELU)
+            return rectified
+
+        def z_on_scalar(j0, w):
+            z_planar = ring.tile([P, PACK, w], BF16, name="z_planar")
+            for t in range(PACK):
+                rectified = sum_taps(j0, w, t)
+                back = psum.tile([P, w], F32, name="back")
+                for b in range(0, w, P):
+                    nc.tensor.transpose(back[:, b : b + P], rectified[:, b : b + P], ident[:])
+                nc.scalar.activation(z_planar[:, t, :], back[:], COPY, scale=gate[:, t : t + 1])
+            z_b = ring.tile([P, w, PACK], BF16, name="z_b", align_bytes=64)
+            nc.scalar.copy(z_b[:], z_planar[:].rearrange("p t w -> p w t"))
+            return z_b
+
+        def z_on_vector(j0, w):
+            rect = [sum_taps(j0, w, 0), sum_taps(j0, w, 1)]
+            back = psum.tile([P, PACK, w], F32, name="back")
+            for t in range(PACK):
+                nc.tensor.transpose(back[:, t, :], rect[t][:], ident[:])
+                if t + 2 < PACK:
+                    rect.append(sum_taps(j0, w, t + 2))
+            z_b = ring.tile([P, w, PACK], BF16, name="z_b", align_bytes=64)
+            nc.vector.tensor_tensor(
+                z_b[:],
+                back[:].rearrange("p t w -> p w t"),
+                gate[:].unsqueeze(1).to_broadcast([P, w, PACK]),
+                MULT,
+            )
+            return z_b
+
+        def second_product(j0, w, z_b, last):
+            cols = slice(j0, j0 + w)
+            nc.vector.quantize_mx(
+                out=z_codes[:, cols].bitcast(FP8X4), scales=z_s[:, cols], in_=z_b[:].rearrange("p w t -> p (w t)")
+            )
+            o_f = ring.tile([P, PACK, w], F32, name="o_f")
+            o_b = ring.tile([P, w, PACK], BF16, name="o_b", align_bytes=64)
+            for b in range(0, w, P):
+                o_bank = psum.tile([P, PACK, P], F32, name="o_bank")
+                for t in range(PACK):
+                    rows = slice(P * t, P * (t + 1))
+                    nc.tensor.matmul_mx(
+                        out=o_bank[:, t, :],
+                        lhsT=w1w_dealt[:, rows].bitcast(FP8X4),
+                        lhsT_scale=w1s_dealt[:, rows],
+                        rhs=z_codes[:, j0 + b : j0 + b + P].bitcast(FP8X4),
+                        rhs_scale=z_s[:, j0 + b : j0 + b + P],
+                        start=True,
+                        stop=True,
+                    )
+                woven = o_bank[:].rearrange("p t w -> p w t")
+                if last:
+                    nc.vector.tensor_copy(o_b[:, b : b + P, :], woven)
+                else:
+                    nc.scalar.copy(o_b[:, b : b + P, :], woven)
+                nc.scalar.copy(o_f[:, :, b : b + P], o_bank[:])
+            nc.sync.dma_start(out_rows[:, :, cols], o_f[:])
+            return o_b
+
+        def planes(j0, w, o_b):
+            cols = slice(j0, j0 + w)
+            nc.vector.quantize_mx(
+                out=o_codes[:, cols].bitcast(FP8X4), scales=o_s[:, cols], in_=o_b[:].rearrange("p w t -> p (w t)")
+            )
+            nc.sync.dma_start(out_words[:, cols], o_codes[:, cols].bitcast(I32))
+
+        (a0, aw), (b0, bw), (c0, cw) = STAGES
+        z_a = z_on_scalar(a0, aw)
+        z_b2 = z_on_scalar(b0, bw)
+        o_a = second_product(a0, aw, z_a, False)
+        z_c = z_on_vector(c0, cw)
+        o_b2 = second_product(b0, bw, z_b2, False)
+        planes(a0, aw, o_a)
+        o_c = second_product(c0, cw, z_c, True)
+        planes(b0, bw, o_b2)
+        planes(c0, cw, o_c)
+        for q in range(4):
+            queue = nc.sync if q % 2 == 0 else nc.scalar
+            queue.dma_start(out_2[0][4 * q : 4 * q + 4, :].bitcast(I32), o_s[32 * q : 32 * q + 4, :].bitcast(I32))

@@ -13,6 +13,8 @@ FP8X4 = mybir.dt.float8_e4m3fn_x4
 MULT = mybir.AluOpType.mult
 RELU = mybir.ActivationFunctionType.Relu
 COPY = mybir.ActivationFunctionType.Copy
+ABS = mybir.ActivationFunctionType.Abs
+SIGN = mybir.ActivationFunctionType.Sign
 
 P = 128
 PACK = 4
@@ -22,7 +24,7 @@ H = 512
 FLOPS = 2 * 2 * 512 * 512 * 512
 
 WA_PIECES = ((0, 256), (256, 128), (384, 128))
-STAGES = ((0, 256), (256, 128), (384, 128))
+STAGES = ((0, 384), (384, 128))
 
 
 def tile_picked_feattap_relu_po_kernel(
@@ -46,23 +48,30 @@ def tile_picked_feattap_relu_po_kernel(
         wa_raw = [keep.tile([P, PACK, w], F32, name=f"wa_raw{i}") for i, (j0, w) in enumerate(WA_PIECES)]
 
         nc.gpsimd.memset(x_s[:].bitcast(I32), 0)
-        nc.vector.memset(w1_s[:].bitcast(I32), 0)
+        nc.gpsimd.memset(w1_s[:].bitcast(I32), 0)
         make_identity(nc, ident[:])
 
+        wa_rows = wa.rearrange("(p j) n -> p j n", j=PACK)
+
+        def load_wa(i):
+            j0, w = WA_PIECES[i]
+            nc.sync.dma_start(wa_raw[i][:], wa_rows[:, :, j0 : j0 + w])
+
         nc.sync.dma_start(picks[:], offs)
+        load_wa(0)
         for q in range(4):
             nc.sync.dma_start(x_s[32 * q : 32 * q + 4, :].bitcast(I32), x_scales[0][4 * q : 4 * q + 4, :].bitcast(I32))
         nc.sync.dma_start(x_w[:].bitcast(I32), x_words[0].rearrange("p n t -> p (n t)").bitcast(I32))
-        wa_rows = wa.rearrange("(p j) n -> p j n", j=PACK)
-        for i, (j0, w) in enumerate(WA_PIECES):
-            nc.sync.dma_start(wa_raw[i][:], wa_rows[:, :, j0 : j0 + w])
+        load_wa(1)
+        load_wa(2)
+        nc.sync.dma_start(gate[:], gt.rearrange("(p t) o -> p (t o)", t=PACK))
+        for k, f in enumerate((f1, f2, f3)):
+            nc.sync.dma_start(taps[k][:], f)
         nc.sync.dma_start(w1_w[:], w1_words[0].rearrange("p n t -> p (n t)").bitcast(I32))
+        for k, c in enumerate((c1, c2, c3)):
+            nc.sync.dma_start(coef[k][:], c)
         for q in range(4):
             nc.gpsimd.dma_start(w1_s[32 * q : 32 * q + 4, :].bitcast(I32), w1_scales[0][4 * q : 4 * q + 4, :].bitcast(I32))
-        for k, (f, c) in enumerate(((f1, c1), (f2, c2), (f3, c3))):
-            nc.sync.dma_start(taps[k][:], f)
-            nc.sync.dma_start(coef[k][:], c)
-        nc.gpsimd.dma_start(gate[:], gt.rearrange("(p t) o -> p (t o)", t=PACK))
 
         xs_picked = keep.tile([P, S], U8, name="xs_picked", align_bytes=64)
         xs_dealt = keep.tile([P, S], U8, name="xs_dealt", align_bytes=64)
@@ -76,9 +85,9 @@ def tile_picked_feattap_relu_po_kernel(
         wa_codes = keep.tile([P, H], U32, name="wa_codes", align_bytes=64)
         wa_s = keep.tile([P, H], U8, name="wa_s", align_bytes=64)
         wa_b = [keep.tile([P, w, PACK], BF16, name=f"wa_b{i}", align_bytes=64) for i, (j0, w) in enumerate(WA_PIECES)]
-        nc.scalar.copy(wa_b[0][:], wa_raw[0][:].rearrange("p j w -> p w j"))
-        for i in (1, 2):
-            nc.vector.tensor_copy(wa_b[i][:], wa_raw[i][:].rearrange("p j w -> p w j"))
+        for i in (0, 1):
+            nc.scalar.copy(wa_b[i][:], wa_raw[i][:].rearrange("p j w -> p w j"))
+        nc.vector.tensor_copy(wa_b[2][:], wa_raw[2][:].rearrange("p j w -> p w j"))
         for i, (j0, w) in enumerate(WA_PIECES):
             nc.vector.quantize_mx(
                 out=wa_codes[:, j0 : j0 + w].bitcast(FP8X4),
@@ -86,21 +95,29 @@ def tile_picked_feattap_relu_po_kernel(
                 in_=wa_b[i][:].rearrange("p w j -> p (w j)"),
             )
 
+        gate_size = keep.tile([P, PACK], F32, name="gate_size")
+        gate_sign = keep.tile([P, PACK], BF16, name="gate_sign")
+        nc.scalar.activation(gate_size[:], gate[:], ABS)
+        nc.scalar.activation(gate_sign[:], gate[:], SIGN)
+
         y = [keep.tile([P, H], F32, name=f"y{t}") for t in range(PACK)]
         for t in range(PACK):
-            y_bank = psum.tile([P, H], F32, name="y_bank")
             rows = slice(P * t, P * (t + 1))
-            for j0, w in WA_PIECES if t == 0 else ((0, H),):
-                nc.tensor.matmul_mx(
-                    out=y_bank[:, j0 : j0 + w],
-                    lhsT=xw_dealt[:, rows].bitcast(FP8X4),
-                    lhsT_scale=xs_dealt[:, rows],
-                    rhs=wa_codes[:, j0 : j0 + w].bitcast(FP8X4),
-                    rhs_scale=wa_s[:, j0 : j0 + w],
-                    start=True,
-                    stop=True,
-                )
-            nc.scalar.copy(y[t][:], y_bank[:])
+            for pieces in (WA_PIECES[:1], WA_PIECES[1:]) if t == 0 else (((0, H),),):
+                lo = pieces[0][0]
+                hi = pieces[-1][0] + pieces[-1][1]
+                y_bank = psum.tile([P, hi - lo], F32, name="y_bank", tag="turned", bufs=4)
+                for j0, w in pieces:
+                    nc.tensor.matmul_mx(
+                        out=y_bank[:, j0 - lo : j0 - lo + w],
+                        lhsT=xw_dealt[:, rows].bitcast(FP8X4),
+                        lhsT_scale=xs_dealt[:, rows],
+                        rhs=wa_codes[:, j0 : j0 + w].bitcast(FP8X4),
+                        rhs_scale=wa_s[:, j0 : j0 + w],
+                        start=True,
+                        stop=True,
+                    )
+                nc.scalar.activation(y[t][:, lo:hi], y_bank[:], COPY, scale=gate_size[:, t : t + 1])
 
         w1w_dealt = keep.tile([P, S], I32, name="w1w_dealt", align_bytes=64)
         w1s_dealt = keep.tile([P, S], U8, name="w1s_dealt", align_bytes=64)
@@ -118,64 +135,57 @@ def tile_picked_feattap_relu_po_kernel(
         out_rows = out_0.rearrange("(p t) n -> p t n", t=PACK)
         out_words = out_1[0].rearrange("p n t -> p (n t)").bitcast(I32)
 
-        def sum_taps(j0, w, t):
+        def weighted_taps(j0, w, t):
             terms = []
             for k in range(3):
-                term = ring.tile([P, w], F32, name="term", bufs=6)
+                term = ring.tile([P, w], F32, name="term", bufs=9)
                 nc.vector.tensor_tensor(
                     term[:], y[t][:].indirect(taps[k][:, j0 // 16 : (j0 + w) // 16]), coef[k][:, j0 : j0 + w], MULT
                 )
                 terms.append(term)
-            turned = psum.tile([P, w], F32, name="turned")
-            for b in range(0, w, P):
-                for k in range(3):
-                    nc.tensor.matmul(
-                        turned[:, b : b + P],
-                        terms[k][:, b : b + P],
-                        ident[:],
-                        start=(k == 0),
-                        stop=(k == 2),
-                        is_transpose=True,
-                    )
-            rectified = ring.tile([P, w], F32, name="rectified")
-            nc.scalar.activation(rectified[:], turned[:], RELU)
-            return rectified
+            return terms
 
-        def z_on_scalar(j0, w):
-            z_planar = ring.tile([P, PACK, w], BF16, name="z_planar")
-            for t in range(PACK):
-                rectified = sum_taps(j0, w, t)
-                back = psum.tile([P, w], F32, name="back")
-                for b in range(0, w, P):
-                    nc.tensor.transpose(back[:, b : b + P], rectified[:, b : b + P], ident[:])
-                nc.scalar.activation(z_planar[:, t, :], back[:], COPY, scale=gate[:, t : t + 1])
-            z_b = ring.tile([P, w, PACK], BF16, name="z_b", align_bytes=64)
-            nc.scalar.copy(z_b[:], z_planar[:].rearrange("p t w -> p w t"))
-            return z_b
+        def groups(w):
+            return [(g0, min(2 * P, w - g0)) for g0 in range(0, w, 2 * P)]
 
-        def z_on_vector(j0, w):
-            rect = [sum_taps(j0, w, 0), sum_taps(j0, w, 1)]
-            back = psum.tile([P, PACK, w], F32, name="back")
-            for t in range(PACK):
-                nc.tensor.transpose(back[:, t, :], rect[t][:], ident[:])
-                if t + 2 < PACK:
-                    rect.append(sum_taps(j0, w, t + 2))
+        def rectified_sums(j0, w):
+            backs = [psum.tile([P, 2, gw], F32, name="back") for g0, gw in groups(w)]
+            for u in range(2):
+                turned = [psum.tile([P, gw // P, 2, P], F32, name="turned", bufs=4) for g0, gw in groups(w)]
+                for e in range(2):
+                    terms = weighted_taps(j0, w, 2 * u + e)
+                    for b in range(w // P):
+                        for k in range(3):
+                            nc.tensor.matmul(
+                                turned[b // 2][:, b % 2, e, :],
+                                terms[k][:, P * b : P * (b + 1)],
+                                ident[:],
+                                start=(k == 0),
+                                stop=(k == 2),
+                                is_transpose=True,
+                            )
+                for g, (g0, gw) in enumerate(groups(w)):
+                    pairs = ring.tile([P, gw // P, P, 2], BF16, name="pairs", bufs=3)
+                    nc.scalar.activation(pairs[:], turned[g][:].rearrange("j b e p -> j b p e"), RELU)
+                    pair_words = pairs[:].rearrange("j b p e -> j b (p e)").bitcast(F32)
+                    for b in range(gw // P):
+                        nc.tensor.transpose(backs[g][:, u, P * b : P * (b + 1)], pair_words[:, b, :], ident[:])
+            return backs
+
+        def second_product(j0, w, back, last):
+            cols = slice(j0, j0 + w)
             z_b = ring.tile([P, w, PACK], BF16, name="z_b", align_bytes=64)
             nc.vector.tensor_tensor(
-                z_b[:],
-                back[:].rearrange("p t w -> p w t"),
-                gate[:].unsqueeze(1).to_broadcast([P, w, PACK]),
+                z_b[:].rearrange("p j (u e) -> p j u e", u=2),
+                back[:].bitcast(BF16).rearrange("p u (j e) -> p j u e", e=2),
+                gate_sign[:].rearrange("p (u e) -> p u e", u=2).unsqueeze(1).to_broadcast([P, w, 2, 2]),
                 MULT,
             )
-            return z_b
-
-        def second_product(j0, w, z_b, last):
-            cols = slice(j0, j0 + w)
             nc.vector.quantize_mx(
                 out=z_codes[:, cols].bitcast(FP8X4), scales=z_s[:, cols], in_=z_b[:].rearrange("p w t -> p (w t)")
             )
-            o_f = ring.tile([P, PACK, w], F32, name="o_f")
-            o_b = ring.tile([P, w, PACK], BF16, name="o_b", align_bytes=64)
+            o_f = ring.tile([P, PACK, w], F32, name="o_f", bufs=3)
+            o_b = ring.tile([P, w, PACK], BF16, name="o_b", align_bytes=64, bufs=3)
             for b in range(0, w, P):
                 o_bank = psum.tile([P, PACK, P], F32, name="o_bank")
                 for t in range(PACK):
@@ -205,16 +215,14 @@ def tile_picked_feattap_relu_po_kernel(
             )
             nc.sync.dma_start(out_words[:, cols], o_codes[:, cols].bitcast(I32))
 
-        (a0, aw), (b0, bw), (c0, cw) = STAGES
-        z_a = z_on_scalar(a0, aw)
-        z_b2 = z_on_scalar(b0, bw)
-        o_a = second_product(a0, aw, z_a, False)
-        z_c = z_on_vector(c0, cw)
-        o_b2 = second_product(b0, bw, z_b2, False)
-        planes(a0, aw, o_a)
-        o_c = second_product(c0, cw, z_c, True)
-        planes(b0, bw, o_b2)
-        planes(c0, cw, o_c)
+        (a0, aw), (b0, bw) = STAGES
+        backs_a = rectified_sums(a0, aw)
+        rounded = [second_product(a0 + g0, gw, backs_a[g], False) for g, (g0, gw) in enumerate(groups(aw))]
+        backs_b = rectified_sums(b0, bw)
+        last_rounded = second_product(b0, bw, backs_b[0], True)
+        for g, (g0, gw) in enumerate(groups(aw)):
+            planes(a0 + g0, gw, rounded[g])
+        planes(b0, bw, last_rounded)
         for q in range(4):
             queue = nc.sync if q % 2 == 0 else nc.scalar
             queue.dma_start(out_2[0][4 * q : 4 * q + 4, :].bitcast(I32), o_s[32 * q : 32 * q + 4, :].bitcast(I32))

from contextlib import ExitStack

import concourse.mybir as mybir
from concourse.masks import make_identity

F32 = mybir.dt.float32
BF16 = mybir.dt.bfloat16
I32 = mybir.dt.int32
U32 = mybir.dt.uint32
U16 = mybir.dt.uint16
U8 = mybir.dt.uint8
FP8X4 = mybir.dt.float8_e4m3fn_x4
MULT = mybir.AluOpType.mult
RELU = mybir.ActivationFunctionType.Relu
COPY = mybir.ActivationFunctionType.Copy
ABS = mybir.ActivationFunctionType.Abs
SIGN = mybir.ActivationFunctionType.Sign

P = 128
PACK = 4
T = 2048
S = 512
H = 512
FLOPS = 2 * 2 * 512 * 512 * 512

WA_PIECES = ((0, 256), (256, 128), (384, 128))
STAGES = ((0, 384), (384, 128))


def tile_picked_feattap_relu_po_kernel(
    tc, x_words, x_scales, wa, c1, c2, c3, gt, w1_words, w1_scales, offs, f1, f2, f3, out_0, out_1, out_2
):
    nc = tc.nc
    with ExitStack() as ctx:
        keep = ctx.enter_context(tc.tile_pool(name="keep", bufs=1))
        ring = ctx.enter_context(tc.tile_pool(name="ring", bufs=2))
        psum = ctx.enter_context(tc.psum_pool(name="psum", bufs=2))

        picks = keep.tile([P, S // 16], U16, name="picks")
        taps = [keep.tile([P, H // 16], U16, name=f"taps{k}") for k in range(3)]
        x_w = keep.tile([P, T], U32, name="x_w", align_bytes=64)
        x_s = keep.tile([P, T], U8, name="x_s", align_bytes=64)
        w1_w = keep.tile([P, S], I32, name="w1_w", align_bytes=64)
        w1_s = keep.tile([P, S], U8, name="w1_s", align_bytes=64)
        coef = [keep.tile([P, H], F32, name=f"coef{k}") for k in range(3)]
        gate = keep.tile([P, PACK], F32, name="gate")
        ident = keep.tile([P, P], F32, name="ident")
        wa_raw = [keep.tile([P, PACK, w], F32, name=f"wa_raw{i}") for i, (j0, w) in enumerate(WA_PIECES)]

        nc.gpsimd.memset(x_s[:].bitcast(I32), 0)
        nc.gpsimd.memset(w1_s[:].bitcast(I32), 0)
        make_identity(nc, ident[:])

        wa_rows = wa.rearrange("(p j) n -> p j n", j=PACK)

        def load_wa(i):
            j0, w = WA_PIECES[i]
            nc.sync.dma_start(wa_raw[i][:], wa_rows[:, :, j0 : j0 + w])

        nc.sync.dma_start(picks[:], offs)
        load_wa(0)
        for q in range(4):
            nc.sync.dma_start(x_s[32 * q : 32 * q + 4, :].bitcast(I32), x_scales[0][4 * q : 4 * q + 4, :].bitcast(I32))
        nc.sync.dma_start(x_w[:].bitcast(I32), x_words[0].rearrange("p n t -> p (n t)").bitcast(I32))
        load_wa(1)
        load_wa(2)
        nc.sync.dma_start(gate[:], gt.rearrange("(p t) o -> p (t o)", t=PACK))
        for k, f in enumerate((f1, f2, f3)):
            nc.sync.dma_start(taps[k][:], f)
        nc.sync.dma_start(w1_w[:], w1_words[0].rearrange("p n t -> p (n t)").bitcast(I32))
        for k, c in enumerate((c1, c2, c3)):
            nc.sync.dma_start(coef[k][:], c)
        for q in range(4):
            nc.gpsimd.dma_start(w1_s[32 * q : 32 * q + 4, :].bitcast(I32), w1_scales[0][4 * q : 4 * q + 4, :].bitcast(I32))

        xs_picked = keep.tile([P, S], U8, name="xs_picked", align_bytes=64)
        xs_dealt = keep.tile([P, S], U8, name="xs_dealt", align_bytes=64)
        xw_dealt = keep.tile([P, S], U32, name="xw_dealt", align_bytes=64)
        nc.vector.tensor_copy(xs_picked[:], x_s[:].indirect(picks[:]))
        nc.vector.tensor_copy(
            xs_dealt[:].rearrange("p (t m) -> p t m", t=PACK), xs_picked[:].rearrange("p (m t) -> p t m", t=PACK)
        )
        nc.vector.tensor_copy(xw_dealt[:].rearrange("p (t m) -> p m t", t=PACK), x_w[:].indirect(picks[:]))

        wa_codes = keep.tile([P, H], U32, name="wa_codes", align_bytes=64)
        wa_s = keep.tile([P, H], U8, name="wa_s", align_bytes=64)
        wa_b = [keep.tile([P, w, PACK], BF16, name=f"wa_b{i}", align_bytes=64) for i, (j0, w) in enumerate(WA_PIECES)]
        for i in (0, 1):
            nc.scalar.copy(wa_b[i][:], wa_raw[i][:].rearrange("p j w -> p w j"))
        nc.vector.tensor_copy(wa_b[2][:], wa_raw[2][:].rearrange("p j w -> p w j"))
        for i, (j0, w) in enumerate(WA_PIECES):
            nc.vector.quantize_mx(
                out=wa_codes[:, j0 : j0 + w].bitcast(FP8X4),
                scales=wa_s[:, j0 : j0 + w],
                in_=wa_b[i][:].rearrange("p w j -> p (w j)"),
            )

        gate_size = keep.tile([P, PACK], F32, name="gate_size")
        gate_sign = keep.tile([P, PACK], BF16, name="gate_sign")
        nc.scalar.activation(gate_size[:], gate[:], ABS)
        nc.scalar.activation(gate_sign[:], gate[:], SIGN)

        y = [keep.tile([P, H], F32, name=f"y{t}") for t in range(PACK)]
        for t in range(PACK):
            rows = slice(P * t, P * (t + 1))
            for pieces in (WA_PIECES[:1], WA_PIECES[1:]) if t == 0 else (((0, H),),):
                lo = pieces[0][0]
                hi = pieces[-1][0] + pieces[-1][1]
                y_bank = psum.tile([P, hi - lo], F32, name="y_bank", tag="turned", bufs=4)
                for j0, w in pieces:
                    nc.tensor.matmul_mx(
                        out=y_bank[:, j0 - lo : j0 - lo + w],
                        lhsT=xw_dealt[:, rows].bitcast(FP8X4),
                        lhsT_scale=xs_dealt[:, rows],
                        rhs=wa_codes[:, j0 : j0 + w].bitcast(FP8X4),
                        rhs_scale=wa_s[:, j0 : j0 + w],
                        start=True,
                        stop=True,
                    )
                nc.scalar.activation(y[t][:, lo:hi], y_bank[:], COPY, scale=gate_size[:, t : t + 1])

        w1w_dealt = keep.tile([P, S], I32, name="w1w_dealt", align_bytes=64)
        w1s_dealt = keep.tile([P, S], U8, name="w1s_dealt", align_bytes=64)
        nc.vector.tensor_copy(
            w1w_dealt[:].rearrange("p (t m) -> p t m", t=PACK), w1_w[:].rearrange("p (m t) -> p t m", t=PACK)
        )
        nc.vector.tensor_copy(
            w1s_dealt[:].rearrange("p (t m) -> p t m", t=PACK), w1_s[:].rearrange("p (m t) -> p t m", t=PACK)
        )

        z_codes = keep.tile([P, H], U32, name="z_codes", align_bytes=64)
        z_s = keep.tile([P, H], U8, name="z_s", align_bytes=64)
        o_codes = keep.tile([P, H], U32, name="o_codes", align_bytes=64)
        o_s = keep.tile([P, H], U8, name="o_s", align_bytes=64)
        out_rows = out_0.rearrange("(p t) n -> p t n", t=PACK)
        out_words = out_1[0].rearrange("p n t -> p (n t)").bitcast(I32)

        def weighted_taps(j0, w, t):
            terms = []
            for k in range(3):
                term = ring.tile([P, w], F32, name="term", bufs=9)
                nc.vector.tensor_tensor(
                    term[:], y[t][:].indirect(taps[k][:, j0 // 16 : (j0 + w) // 16]), coef[k][:, j0 : j0 + w], MULT
                )
                terms.append(term)
            return terms

        def groups(w):
            return [(g0, min(2 * P, w - g0)) for g0 in range(0, w, 2 * P)]

        def rectified_sums(j0, w):
            backs = [psum.tile([P, 2, gw], F32, name="back") for g0, gw in groups(w)]
            for u in range(2):
                turned = [psum.tile([P, gw // P, 2, P], F32, name="turned", bufs=4) for g0, gw in groups(w)]
                for e in range(2):
                    terms = weighted_taps(j0, w, 2 * u + e)
                    for b in range(w // P):
                        for k in range(3):
                            nc.tensor.matmul(
                                turned[b // 2][:, b % 2, e, :],
                                terms[k][:, P * b : P * (b + 1)],
                                ident[:],
                                start=(k == 0),
                                stop=(k == 2),
                                is_transpose=True,
                            )
                for g, (g0, gw) in enumerate(groups(w)):
                    pairs = ring.tile([P, gw // P, P, 2], BF16, name="pairs", bufs=3)
                    nc.scalar.activation(pairs[:], turned[g][:].rearrange("j b e p -> j b p e"), RELU)
                    pair_words = pairs[:].rearrange("j b p e -> j b (p e)").bitcast(F32)
                    for b in range(gw // P):
                        nc.tensor.transpose(backs[g][:, u, P * b : P * (b + 1)], pair_words[:, b, :], ident[:])
            return backs

        def second_product(j0, w, back, last):
            cols = slice(j0, j0 + w)
            z_b = ring.tile([P, w, PACK], BF16, name="z_b", align_bytes=64)
            nc.vector.tensor_tensor(
                z_b[:].rearrange("p j (u e) -> p j u e", u=2),
                back[:].bitcast(BF16).rearrange("p u (j e) -> p j u e", e=2),
                gate_sign[:].rearrange("p (u e) -> p u e", u=2).unsqueeze(1).to_broadcast([P, w, 2, 2]),
                MULT,
            )
            nc.vector.quantize_mx(
                out=z_codes[:, cols].bitcast(FP8X4), scales=z_s[:, cols], in_=z_b[:].rearrange("p w t -> p (w t)")
            )
            o_f = ring.tile([P, PACK, w], F32, name="o_f", bufs=3)
            o_b = ring.tile([P, w, PACK], BF16, name="o_b", align_bytes=64, bufs=3)
            for b in range(0, w, P):
                o_bank = psum.tile([P, PACK, P], F32, name="o_bank")
                for t in range(PACK):
                    rows = slice(P * t, P * (t + 1))
                    nc.tensor.matmul_mx(
                        out=o_bank[:, t, :],
                        lhsT=w1w_dealt[:, rows].bitcast(FP8X4),
                        lhsT_scale=w1s_dealt[:, rows],
                        rhs=z_codes[:, j0 + b : j0 + b + P].bitcast(FP8X4),
                        rhs_scale=z_s[:, j0 + b : j0 + b + P],
                        start=True,
                        stop=True,
                    )
                woven = o_bank[:].rearrange("p t w -> p w t")
                if last:
                    nc.vector.tensor_copy(o_b[:, b : b + P, :], woven)
                else:
                    nc.scalar.copy(o_b[:, b : b + P, :], woven)
                nc.scalar.copy(o_f[:, :, b : b + P], o_bank[:])
            nc.sync.dma_start(out_rows[:, :, cols], o_f[:])
            return o_b

        def planes(j0, w, o_b):
            cols = slice(j0, j0 + w)
            nc.vector.quantize_mx(
                out=o_codes[:, cols].bitcast(FP8X4), scales=o_s[:, cols], in_=o_b[:].rearrange("p w t -> p (w t)")
            )
            nc.sync.dma_start(out_words[:, cols], o_codes[:, cols].bitcast(I32))

        (a0, aw), (b0, bw) = STAGES
        backs_a = rectified_sums(a0, aw)
        rounded = [second_product(a0 + g0, gw, backs_a[g], False) for g, (g0, gw) in enumerate(groups(aw))]
        backs_b = rectified_sums(b0, bw)
        last_rounded = second_product(b0, bw, backs_b[0], True)
        for g, (g0, gw) in enumerate(groups(aw)):
            planes(a0 + g0, gw, rounded[g])
        planes(b0, bw, last_rounded)
        for q in range(4):
            queue = nc.sync if q % 2 == 0 else nc.scalar
            queue.dma_start(out_2[0][4 * q : 4 * q + 4, :].bitcast(I32), o_s[32 * q : 32 * q + 4, :].bitcast(I32))
